import numpy as np
import ml_dtypes


def mxq(x, axis, fmt="e4m3"):
    dtype, down = {"e4m3": (ml_dtypes.float8_e4m3fn, 7), "e5m2": (ml_dtypes.float8_e5m2, 14)}[fmt]
    v = np.moveaxis(np.asarray(x, np.float32).astype(ml_dtypes.bfloat16).astype(np.float64), axis, -1)
    blocks = v.reshape(v.shape[:-1] + (-1, 32))
    amax = np.abs(blocks).max(-1, keepdims=True)
    byte = np.maximum(np.where(amax > 0, np.frexp(amax)[1] - 1 + 127, 0) - down, 1)
    scale = np.exp2(byte - 127.0)
    codes = (blocks / scale).astype(np.float32).astype(dtype).astype(np.float64)
    return np.moveaxis((codes * scale).reshape(v.shape), -1, axis)


WIDE = False


def mx_kscale(k):
    if not WIDE:
        return np.ones(k)
    levels = np.array([10, -10, 5, -5, 0])
    if k % 512:
        return np.exp2(np.random.permutation(np.resize(levels, k // 32))).repeat(32)
    a = np.empty((k // 512, 16))
    for p in range(k // 512):
        a[p, :8] = np.random.permutation(np.resize(levels, 8))
        for g in range(8):
            far = levels[np.abs(levels - a[p, g]) >= 10]
            a[p, g + 8] = far[np.random.randint(len(far))]
    return np.exp2(a.ravel()).repeat(32)


BF16 = ml_dtypes.bfloat16


def bf(x):
    return np.asarray(x, np.float32).astype(BF16)


def f64(x):
    return np.asarray(x).astype(np.float64)


E2M1 = np.array([0.0, 0.5, 1.0, 1.5, 2.0, 3.0, 4.0, 6.0, -0.0, -0.5, -1.0, -1.5, -2.0, -3.0, -4.0, -6.0])


def pack_weight(w, fmt):
    k, n = w.shape
    w = f64(bf(w)).reshape(k // 32, 32, n)
    amax = np.abs(w).max(1)
    if fmt == "e4m3":
        byte = np.frexp(amax)[1] - 1 + 127 - 7
    else:
        mant, ex = np.frexp(amax / 6.0)
        byte = np.where(mant > 0.5, ex, ex - 1) + 127
    byte = np.clip(np.where(amax > 0, byte, 1), 1, 254)
    scaled = (w * np.exp2(127.0 - byte)[:, None, :]).reshape(k, n).astype(np.float32)
    by_word = np.ascontiguousarray(scaled.reshape(k // 512, 128, 4, n).transpose(0, 1, 3, 2))
    if fmt == "e4m3":
        words = by_word.astype(ml_dtypes.float8_e4m3fn).view(np.uint8)
    else:
        c = by_word.astype(ml_dtypes.float4_e2m1fn).view(np.uint8) & 0xF
        words = c[..., 0::2] | (c[..., 1::2] << 4)
    return np.ascontiguousarray(words), np.ascontiguousarray(byte.astype(np.uint8).reshape(k // 512, 16, n))


def unpack_weight(words, scales, fmt):
    g, p, n, _ = words.shape
    if fmt == "e4m3":
        vals = np.ascontiguousarray(words).view(ml_dtypes.float8_e4m3fn).astype(np.float64)
    else:
        nib = np.empty((g, p, n, 4), np.uint8)
        nib[..., 0::2] = words & 0xF
        nib[..., 1::2] = words >> 4
        vals = E2M1[nib]
    vals = vals * np.repeat(np.exp2(scales.astype(np.float64) - 127.0), 8, axis=1)[..., None]
    return vals.transpose(0, 1, 3, 2).reshape(g * 512, n)
def pack4(w):
    words, scales = pack_weight(w, "e2m1")
    return words.reshape(words.shape[0], 128, -1), scales


def unpack4(words, scales):
    return unpack_weight(words.reshape(words.shape[0], 128, -1, 2), scales, "e2m1")


M, F, D, I = 1536, 512, 1024, 2048


def setup_inputs():
    s, t, v = mx_kscale(F), mx_kscale(D), mx_kscale(I)
    x = bf(np.random.standard_normal((M, F)) * s)
    w_words, w_scales = pack4(np.random.standard_normal((F, D)) / np.sqrt(F) / s[:, None] * t)
    q = bf(np.random.standard_normal((I, D)) * v[:, None] / t)
    c = bf(np.exp(0.5 * np.random.standard_normal(I)) / I / v ** 2)
    return {"x": x, "w_words": w_words, "w_scales": w_scales, "q": q, "c": c}


def reference(x, w_words, w_scales, q, c):
    qf = f64(q)
    p = mxq(f64(x), 1, "e4m3") @ unpack4(w_words, w_scales)
    qc = qf * f64(c)[:, None]
    g = mxq(qc, 0, "e4m3").T @ mxq(qf, 0, "e4m3")
    r = mxq(p, 1, "e4m3") @ mxq(g, 0, "e4m3")
    share = p * r
    loss = share.mean(0)
    return share, loss

@@ -1,0 +1,390 @@
+from contextlib import ExitStack
+
+import concourse.mybir as mybir
+from concourse.masks import make_identity
+
+M, F, D, I = 1536, 512, 1024, 2048
+FLOPS = 2 * M * F * D + 2 * I * D * D + 2 * M * D * D
+
+F32 = mybir.dt.float32
+BF16 = mybir.dt.bfloat16
+I32 = mybir.dt.int32
+U32 = mybir.dt.uint32
+U8 = mybir.dt.uint8
+FP8X4 = mybir.dt.float8_e4m3fn_x4
+FP4X4 = mybir.dt.float4_e2m1fn_x4
+ALU = mybir.AluOpType
+
+P = 128
+HALF = 512
+ITEM_PASSES = I // 512
+TILES = M // P
+VECTOR_COLUMNS = [384, 0, 0, 128, 128, 192, 192, 64]
+PAIRS = 5
+VECTOR_ROUNDS = 1
+
+
+def tile_whole_data_loss_s11_kernel(tc, x, w_words, w_scales, q, c, out_0, out_1):
+    nc = tc.nc
+    with ExitStack() as ctx:
+        keep = ctx.enter_context(tc.tile_pool(name="keep", bufs=1))
+        work = ctx.enter_context(tc.tile_pool(name="work", bufs=2))
+        psum = ctx.enter_context(tc.psum_pool(name="psum", bufs=1))
+        ctx.enter_context(tc.manual_schedule())
+
+        def bank(b, shape):
+            return psum.tile(shape, F32, name="bank%d" % b, tag="bank%d" % b)
+
+        def mx_pair(name, width):
+            codes = keep.tile([P, width], U32, name=name + "_codes", align_bytes=64)
+            scales = keep.tile([P, width], U8, name=name + "_scales", align_bytes=64)
+            return codes, scales
+
+        def quantize(pair, src):
+            nc.vector.quantize_mx(out=pair[0][:].bitcast(FP8X4), scales=pair[1][:], in_=src)
+
+        def mx_matmul(out, lhs, lhs_cols, rhs, rhs_cols, start, stop):
+            nc.tensor.matmul_mx(
+                out=out,
+                lhsT=lhs[0][:, lhs_cols].bitcast(FP8X4),
+                lhsT_scale=lhs[1][:, lhs_cols],
+                rhs=rhs[0][:, rhs_cols].bitcast(FP8X4),
+                rhs_scale=rhs[1][:, rhs_cols],
+                start=start,
+                stop=stop,
+            )
+
+        def cols(n, width=P):
+            return slice(n * width, (n + 1) * width)
+
+        c_sb = keep.tile([P, ITEM_PASSES, 4], BF16, name="c_sb")
+        nc.scalar.dma_start(out=c_sb[:], in_=c.rearrange("(g p j) -> p g j", p=P, j=4))
+
+        q_raw = {}
+        x_raw = {}
+
+        def load_q(h, g):
+            q_raw[h, g] = keep.tile([P, 4, HALF], BF16, name="q_raw%d%d" % (h, g))
+            rows = q[cols(g, 512), cols(h, HALF)]
+            nc.sync.dma_start(out=q_raw[h, g][:], in_=rows.rearrange("(p j) w -> p j w", j=4))
+
+        def load_x(j):
+            x_raw[j] = keep.tile([P, 4, F], BF16, name="x_raw%d" % j)
+            nc.sync.dma_start(out=x_raw[j][:], in_=x[cols(j, 512), :].rearrange("(p m) f -> p m f", m=4))
+
+        ident = keep.tile([P, P], F32, name="ident")
+        make_identity(nc, ident[:])
+        w_plane = keep.tile([P, D], U8, name="w_plane", align_bytes=64)
+        nc.gpsimd.memset(w_plane[:].bitcast(I32), 0)
+        sums = keep.tile([P, P], F32, name="sums")
+        nc.gpsimd.memset(sums[:], 0.0)
+
+        load_q(0, 0)
+        load_q(0, 1)
+        for j in range(2):
+            load_x(j)
+            load_q(0, j + 2)
+        load_x(2)
+        for g in range(ITEM_PASSES):
+            load_q(1, g)
+        w_sb = keep.tile([P, 2 * D], U8, name="w_sb", align_bytes=64)
+        nc.sync.dma_start(out=w_sb[:].bitcast(I32), in_=w_words[0].bitcast(I32))
+        for quad in range(4):
+            nc.sync.dma_start(
+                out=w_plane[32 * quad : 32 * quad + 4, :].bitcast(I32),
+                in_=w_scales[0, 4 * quad : 4 * quad + 4, :].bitcast(I32),
+            )
+
+        q_mx = {}
+        qc_mx = {}
+        q_grouped = {}
+
+        qc_grouped = {}
+        chunks = [(h, g) for h in range(2) for g in range(ITEM_PASSES)]
+        c_run = keep.tile([P, ITEM_PASSES, 8, 4], BF16, name="c_run")
+
+        def interleave_q(k, on_vector):
+            if k >= len(chunks):
+                return
+            if k not in q_grouped:
+                q_grouped[k] = work.tile([P, HALF, 4], BF16, name="q_grouped", bufs=4, align_bytes=64)
+            split = VECTOR_COLUMNS[k]
+            lo, hi, copy = (0, split, nc.vector.tensor_copy) if on_vector else (split, HALF, nc.scalar.copy)
+            if hi > lo:
+                copy(
+                    out=q_grouped[k][:, lo:hi, :].rearrange("p (n i) j -> p n j i", i=4),
+                    in_=q_raw[chunks[k]][:, :, lo:hi].rearrange("p j (n i) -> p n j i", i=4),
+                )
+
+        def quantize_q(k, between=()):
+            h, g = chunks[k]
+            grouped = q_grouped[k]
+            q_mx[h, g] = mx_pair("q%d%d" % (h, g), HALF)
+            qc_mx[h, g] = mx_pair("qc%d%d" % (h, g), HALF)
+            if h == 1:
+                quantize(q_mx[h, g], grouped[:].rearrange("p w j -> p (w j)"))
+            weighted = work.tile([P, HALF, 4], BF16, name="qc_grouped", align_bytes=64)
+            run = c_run[:, g, :, :].rearrange("p r j -> p (r j)")
+            nc.vector.tensor_tensor(
+                out=weighted[:].rearrange("p (t b r) j -> p t b (r j)", t=4, r=8),
+                in0=grouped[:].rearrange("p (b t r) j -> p t b (r j)", t=4, r=8),
+                in1=run.unsqueeze(1).unsqueeze(1).to_broadcast([P, 4, 16, 32]),
+                op=ALU.mult,
+            )
+            interleave_q(k + 1, True)
+            for step in between:
+                step()
+            if h == 0:
+                quantize(q_mx[h, g], grouped[:].rearrange("p w j -> p (w j)"))
+            quantize(qc_mx[h, g], weighted[:].rearrange("p w j -> p (w j)"))
+
+        g_banks = {}
+        g_grouped = {}
+        g_mx = {}
+
+        def gram_pass(h, eh, g, first_bank, banks=range(4)):
+            for n in banks:
+                if g == 0:
+                    g_banks[h, eh, n] = bank(first_bank + n, [P, 4, P])
+                for t in range(4):
+                    mx_matmul(
+                        g_banks[h, eh, n][:, t, :], qc_mx[h, g], cols(t), q_mx[eh, g], cols(n),
+                        start=(g == 0 and t == 0), stop=(g == ITEM_PASSES - 1 and t == 3),
+                    )
+
+        def gram_bank(h, eh, n, first_bank):
+            g_banks[h, eh, n] = bank(first_bank + n, [P, 4, P])
+            for t in range(4):
+                for g in range(ITEM_PASSES):
+                    mx_matmul(
+                        g_banks[h, eh, n][:, t, :], qc_mx[h, g], cols(t), q_mx[eh, g], cols(n),
+                        start=(g == 0), stop=(g == ITEM_PASSES - 1),
+                    )
+
+        def gram_out(h, eh, n, copy):
+            if (h, eh) not in g_grouped:
+                g_grouped[h, eh] = work.tile([P, HALF, 4], BF16, name="g_grouped", bufs=3, align_bytes=64)
+            copy(out=g_grouped[h, eh][:, cols(n), :], in_=g_banks[h, eh, n][:].rearrange("p t e -> p e t"))
+
+        def quantize_g(h, eh):
+            g_mx[h, eh] = mx_pair("g%d%d" % (h, eh), HALF)
+            quantize(g_mx[h, eh], g_grouped[h, eh][:].rearrange("p e t -> p (e t)"))
+
+        x_banks = {}
+        x_grouped = {}
+        x_mx = {}
+
+        def transpose_x(k):
+            x_banks[k] = bank(4 + k % 4, [P, 2, 2, P])
+            for m in range(2):
+                words = x_raw[k // 2][:, 2 * (k % 2) + m, :].bitcast(F32)
+                for u in range(2):
+                    nc.tensor.transpose(x_banks[k][:, m, u, :], words[:, u : F // 2 : 2], ident[:])
+
+        def x_out(k):
+            x_grouped[k] = work.tile([P, 2, P, 4], BF16, name="x_grouped", bufs=3, align_bytes=64)
+            nc.scalar.copy(out=x_grouped[k][:].bitcast(F32), in_=x_banks[k][:].rearrange("p m u a -> p m a u"))
+
+        def quantize_x(k):
+            x_mx[k] = mx_pair("x%d" % k, 2 * P)
+            quantize(x_mx[k], x_grouped[k][:].rearrange("p m a t -> p (m a t)"))
+
+        p_banks = {}
+        p_sb = {}
+        p_words = {}
+        pt_banks = {}
+        pt_grouped = {}
+        p_mx = {}
+
+        def user_factors(s):
+            for eh in range(2):
+                p_banks[s, eh] = bank(eh, [P, HALF])
+                lhs = x_mx[s // 2]
+                nc.tensor.matmul_mx(
+                    out=p_banks[s, eh][:],
+                    lhsT=lhs[0][:, cols(s % 2)].bitcast(FP8X4),
+                    lhsT_scale=lhs[1][:, cols(s % 2)],
+                    rhs=w_sb[:, cols(eh, 2 * HALF)].bitcast(FP4X4),
+                    rhs_scale=w_plane[:, cols(eh, HALF)],
+                    start=True,
+                    stop=True,
+                )
+
+        def round_p(s, h, copy, src):
+            copy(
+                out=p_words[s][:, h, :].rearrange("p (u b r v) -> p u b r v", u=2, r=8, v=2),
+                in_=src.rearrange("p (b u v r) -> p u b r v", u=2, v=2, r=8),
+            )
+
+        def p_out(s):
+            p_sb[s] = work.tile([P, D], F32, name="p_sb", bufs=5)
+            p_words[s] = work.tile([P, 2, HALF], BF16, name="p_words", bufs=3)
+            for eh in range(2):
+                nc.scalar.copy(out=p_sb[s][:, cols(eh, HALF)], in_=p_banks[s, eh][:])
+            for h in range(VECTOR_ROUNDS, 2):
+                round_p(s, h, nc.scalar.copy, p_banks[s, h][:])
+
+        def round_p_first_half(s):
+            for h in range(VECTOR_ROUNDS):
+                round_p(s, h, nc.vector.tensor_copy, p_sb[s][:, cols(h, HALF)])
+
+        def transpose_p(s):
+            pt_banks[s] = bank(2 + s % 2, [P, 2, 2, P])
+            for h in range(2):
+                words = p_words[s][:, h, :].bitcast(F32)
+                for u in range(2):
+                    nc.tensor.transpose(pt_banks[s][:, h, u, :], words[:, cols(u)], ident[:])
+
+        def pt_out(s):
+            pt_grouped[s] = work.tile([P, 2, P, 4], BF16, name="pt_grouped", align_bytes=64)
+            nc.scalar.copy(out=pt_grouped[s][:].bitcast(F32), in_=pt_banks[s][:].rearrange("p h u a -> p h a u"))
+
+        def quantize_p(s):
+            codes = work.tile([P, 2 * P], U32, name="p_codes", bufs=3, align_bytes=64)
+            scales = work.tile([P, 2 * P], U8, name="p_scales", bufs=3, align_bytes=64)
+            p_mx[s] = (codes, scales)
+            quantize(p_mx[s], pt_grouped[s][:].rearrange("p h a t -> p (h a t)"))
+
+        r_banks = {}
+        share = {}
+        pair_sum = {}
+        loss_banks = {}
+        out_tiles = out_0.rearrange("(j p m) e -> j m p e", p=P, m=4)
+
+        def through_gram(s, pieces):
+            for eh in range(2):
+                r_banks[s, eh] = bank(4 + eh, [P, HALF])
+            for eh, lo, hi in pieces:
+                for h in range(2):
+                    mx_matmul(r_banks[s, eh][:, lo:hi], p_mx[s], cols(h), g_mx[h, eh], slice(lo, hi), start=(h == 0), stop=(h == 1))
+
+        def share_out(s, eh):
+            if eh == 0:
+                share[s] = work.tile([P, D], F32, name="share", bufs=5)
+            half = cols(eh, HALF)
+            nc.vector.tensor_tensor(out=share[s][:, half], in0=r_banks[s, eh][:], in1=p_sb[s][:, half], op=ALU.mult)
+
+        def store_share(s, columns):
+            nc.sync.dma_start(out=out_tiles[s // 4, s % 4][:, columns], in_=share[s][:, columns])
+
+        def add_pair(k, eh):
+            half = cols(eh, HALF)
+            pair_sum[k, eh] = work.tile([P, HALF], F32, name="pair_sum")
+            nc.vector.tensor_tensor(out=pair_sum[k, eh][:], in0=share[2 * k][:, half], in1=share[2 * k + 1][:, half], op=ALU.add)
+
+        def add_to_loss(src, eh, first, last):
+            if first:
+                loss_banks[eh] = bank(6 + eh, [P, 4, P])
+            for n in range(4):
+                nc.tensor.matmul(
+                    out=loss_banks[eh][:, n, :], lhsT=src[:, cols(n)], rhs=ident[:], is_transpose=True,
+                    start=(first and n == 0), stop=(last and n == 3),
+                )
+
+        interleave_q(0, True)
+        nc.vector.tensor_copy(out=c_run[:], in_=c_sb[:].unsqueeze(2).to_broadcast([P, ITEM_PASSES, 8, 4]))
+        interleave_q(0, False)
+        for g in range(ITEM_PASSES):
+            interleave_q(g + 1, False)
+            quantize_q(g)
+            if g >= 2:
+                quantize_x(2 * g - 4)
+                quantize_x(2 * g - 3)
+            gram_pass(0, 0, g, 0)
+            if g >= 1:
+                x_out(2 * g - 2)
+                x_out(2 * g - 1)
+            if g < 3:
+                transpose_x(2 * g)
+                transpose_x(2 * g + 1)
+
+        between = [
+            [lambda: quantize_x(4)],
+            [lambda: quantize_x(5)],
+            [],
+            [lambda: quantize_g(0, 0)],
+        ]
+        for g in range(ITEM_PASSES):
+            interleave_q(ITEM_PASSES + g + 1, False)
+            if g < 2:
+                for n in (2 * g, 2 * g + 1):
+                    gram_out(0, 0, n, nc.scalar.copy)
+            quantize_q(ITEM_PASSES + g, between[g])
+            gram_pass(0, 1, g, 4)
+            if g < 2:
+                for earlier in range(g + 1):
+                    gram_pass(1, 0, earlier, 0, (2 * g, 2 * g + 1))
+                if g == 1:
+                    gram_pass(1, 0, 1, 0, (0, 1))
+            else:
+                gram_pass(1, 0, g, 0)
+
+        engines = (nc.scalar.copy, nc.vector.tensor_copy)
+        for n in range(4):
+            gram_out(0, 1, n, engines[n % 2])
+        for n in range(4):
+            gram_out(1, 0, n, engines[n % 2])
+        gram_bank(1, 1, 0, 4)
+        user_factors(0)
+        p_out(0)
+        quantize_g(0, 1)
+        quantize_g(1, 0)
+        gram_bank(1, 1, 1, 4)
+        gram_out(1, 1, 0, nc.vector.tensor_copy)
+        round_p_first_half(0)
+        user_factors(1)
+        p_out(1)
+        gram_bank(1, 1, 2, 4)
+        transpose_p(0)
+        gram_out(1, 1, 1, nc.vector.tensor_copy)
+        round_p_first_half(1)
+        user_factors(2)
+        pt_out(0)
+        p_out(2)
+        gram_bank(1, 1, 3, 4)
+        gram_out(1, 1, 2, nc.vector.tensor_copy)
+        quantize_p(0)
+        transpose_p(1)
+        gram_out(1, 1, 3, nc.vector.tensor_copy)
+        round_p_first_half(2)
+        quantize_g(1, 1)
+
+        halves = [(0, 0, HALF), (1, 0, HALF)]
+        last = TILES - 1
+        for s in range(TILES):
+            paired = 2 <= s < 2 * PAIRS + 2
+            if s + 3 < TILES:
+                user_factors(s + 3)
+            if s + 1 < TILES:
+                pt_out(s + 1)
+            if 0 < s and s + 2 < TILES:
+                round_p_first_half(s + 2)
+            if paired:
+                add_pair(s // 2 - 1, s % 2)
+            if s + 1 < TILES:
+                quantize_p(s + 1)
+            through_gram(s, halves)
+            if s + 3 < TILES:
+                p_out(s + 3)
+            share_out(s, 0)
+            if s == last:
+                store_share(s, cols(0, HALF))
+            share_out(s, 1)
+            store_share(s, cols(1, HALF) if s == last else cols(0, D))
+            if s + 2 < TILES:
+                transpose_p(s + 2)
+            if paired:
+                add_to_loss(pair_sum[s // 2 - 1, s % 2], s % 2, first=(s < 4), last=False)
+            if s - 1 >= 2 * PAIRS and s < last:
+                for eh in range(2):
+                    add_to_loss(share[s - 1][:, cols(eh, HALF)], eh, first=False, last=False)
+
+        for eh in range(2):
+            for s in (last - 1, last):
+                add_to_loss(share[s][:, cols(eh, HALF)], eh, first=False, last=(s == last))
+            nc.vector.tensor_reduce(out=sums[:, cols(eh, 4)], in_=loss_banks[eh][:], axis=mybir.AxisListType.X, op=ALU.add)
+        rows = bank(0, [P, P])
+        nc.tensor.transpose(rows[:], sums[:], ident[:])
+        loss = keep.tile([32, P], F32, name="loss")
+        nc.vector.tensor_scalar(out=loss[:], in0=rows[0:32, :], scalar1=1.0 / M, scalar2=None, op0=ALU.mult)
+        nc.sync.dma_start(out=out_1.rearrange("(n p) -> n p", p=P), in_=loss[0:8, :])

@@ -19,8 +19,16 @@ P = 128
 HALF = 512
 ITEM_PASSES = I // 512
 TILES = M // P
-VECTOR_COLUMNS = [384, 0, 0, 128, 128, 192, 192, 64]
+VECTOR_COLUMNS = [384, 64, 0, 192, 256, 256, 256, 256]
 PAIRS = 5
+X_LAG = 1
+PT_AT = 0
+ALT = 10
+FIRST = [0, 0, 0]
+G11 = [1, 1, 1, 1]
+G00_AT = 2
+W_AT = 2
+G10 = [1, 1, 1, 1]
 VECTOR_ROUNDS = 1
 
 
@@ -57,8 +65,10 @@ def tile_whole_data_loss_s11_kernel(tc, x, w_words, w_scales, q, c, out_0, out_1
         def cols(n, width=P):
             return slice(n * width, (n + 1) * width)
 
-        c_sb = keep.tile([P, ITEM_PASSES, 4], BF16, name="c_sb")
-        nc.scalar.dma_start(out=c_sb[:], in_=c.rearrange("(g p j) -> p g j", p=P, j=4))
+        c_sb = keep.tile([P, ITEM_PASSES - 1, 4], BF16, name="c_sb")
+        c_view = c.rearrange("(g p j) -> p g j", p=P, j=4)
+        c_first = keep.tile([P, 4], BF16, name="c_first")
+        nc.scalar.dma_start(out=c_first[:], in_=c_view[:, 0, :])
 
         q_raw = {}
         x_raw = {}
@@ -79,14 +89,14 @@ def tile_whole_data_loss_s11_kernel(tc, x, w_words, w_scales, q, c, out_0, out_1
         sums = keep.tile([P, P], F32, name="sums")
         nc.gpsimd.memset(sums[:], 0.0)
 
-        load_q(0, 0)
-        load_q(0, 1)
-        for j in range(2):
-            load_x(j)
-            load_q(0, j + 2)
-        load_x(2)
-        for g in range(ITEM_PASSES):
-            load_q(1, g)
+        order = [(0, 0), (0, 1), (0, 2), 0, (0, 3), 1, (1, 0), 2, (1, 1), (1, 2), (1, 3)]
+        for item in order:
+            if isinstance(item, int):
+                load_x(item)
+            else:
+                load_q(*item)
+            if item == (0, 1):
+                nc.sync.dma_start(out=c_sb[:], in_=c_view[:, 1:, :])
         w_sb = keep.tile([P, 2 * D], U8, name="w_sb", align_bytes=64)
         nc.sync.dma_start(out=w_sb[:].bitcast(I32), in_=w_words[0].bitcast(I32))
         for quad in range(4):
@@ -101,13 +111,14 @@ def tile_whole_data_loss_s11_kernel(tc, x, w_words, w_scales, q, c, out_0, out_1
 
         qc_grouped = {}
         chunks = [(h, g) for h in range(2) for g in range(ITEM_PASSES)]
-        c_run = keep.tile([P, ITEM_PASSES, 8, 4], BF16, name="c_run")
+        c_rest = keep.tile([P, ITEM_PASSES - 1, 8, 4], BF16, name="c_rest")
+        c_run = [keep.tile([P, 8, 4], BF16, name="c_run")[:]] + [c_rest[:, g, :, :] for g in range(ITEM_PASSES - 1)]
 
         def interleave_q(k, on_vector):
             if k >= len(chunks):
                 return
             if k not in q_grouped:
-                q_grouped[k] = work.tile([P, HALF, 4], BF16, name="q_grouped", bufs=4, align_bytes=64)
+                q_grouped[k] = work.tile([P, HALF, 4], BF16, name="q_grouped", bufs=5, align_bytes=64)
             split = VECTOR_COLUMNS[k]
             lo, hi, copy = (0, split, nc.vector.tensor_copy) if on_vector else (split, HALF, nc.scalar.copy)
             if hi > lo:
@@ -116,27 +127,23 @@ def tile_whole_data_loss_s11_kernel(tc, x, w_words, w_scales, q, c, out_0, out_1
                     in_=q_raw[chunks[k]][:, :, lo:hi].rearrange("p j (n i) -> p n j i", i=4),
                 )
 
-        def quantize_q(k, between=()):
-            h, g = chunks[k]
-            grouped = q_grouped[k]
-            q_mx[h, g] = mx_pair("q%d%d" % (h, g), HALF)
-            qc_mx[h, g] = mx_pair("qc%d%d" % (h, g), HALF)
-            if h == 1:
-                quantize(q_mx[h, g], grouped[:].rearrange("p w j -> p (w j)"))
-            weighted = work.tile([P, HALF, 4], BF16, name="qc_grouped", align_bytes=64)
-            run = c_run[:, g, :, :].rearrange("p r j -> p (r j)")
+        def quantize_q(k):
+            q_mx[chunks[k]] = mx_pair("q%d" % k, HALF)
+            quantize(q_mx[chunks[k]], q_grouped[k][:].rearrange("p w j -> p (w j)"))
+
+        def weight_q(k):
+            qc_grouped[k] = work.tile([P, HALF, 4], BF16, name="qc_grouped", align_bytes=64)
+            run = c_run[chunks[k][1]].rearrange("p r j -> p (r j)")
             nc.vector.tensor_tensor(
-                out=weighted[:].rearrange("p (t b r) j -> p t b (r j)", t=4, r=8),
-                in0=grouped[:].rearrange("p (b t r) j -> p t b (r j)", t=4, r=8),
+                out=qc_grouped[k][:].rearrange("p (t b r) j -> p t b (r j)", t=4, r=8),
+                in0=q_grouped[k][:].rearrange("p (b t r) j -> p t b (r j)", t=4, r=8),
                 in1=run.unsqueeze(1).unsqueeze(1).to_broadcast([P, 4, 16, 32]),
                 op=ALU.mult,
             )
-            interleave_q(k + 1, True)
-            for step in between:
-                step()
-            if h == 0:
-                quantize(q_mx[h, g], grouped[:].rearrange("p w j -> p (w j)"))
-            quantize(qc_mx[h, g], weighted[:].rearrange("p w j -> p (w j)"))
+
+        def quantize_qc(k):
+            qc_mx[chunks[k]] = mx_pair("qc%d" % k, HALF)
+            quantize(qc_mx[chunks[k]], qc_grouped[k][:].rearrange("p w j -> p (w j)"))
 
         g_banks = {}
         g_grouped = {}
@@ -170,6 +177,15 @@ def tile_whole_data_loss_s11_kernel(tc, x, w_words, w_scales, q, c, out_0, out_1
             g_mx[h, eh] = mx_pair("g%d%d" % (h, eh), HALF)
             quantize(g_mx[h, eh], g_grouped[h, eh][:].rearrange("p e t -> p (e t)"))
 
+        def quantize_g_bank(h, eh, n):
+            if n == 0:
+                g_mx[h, eh] = mx_pair("g%d%d" % (h, eh), HALF)
+            codes, scales = g_mx[h, eh]
+            nc.vector.quantize_mx(
+                out=codes[:, cols(n)].bitcast(FP8X4), scales=scales[:, cols(n)],
+                in_=g_grouped[h, eh][:, cols(n), :].rearrange("p e t -> p (e t)"),
+            )
+
         x_banks = {}
         x_grouped = {}
         x_mx = {}
@@ -182,7 +198,7 @@ def tile_whole_data_loss_s11_kernel(tc, x, w_words, w_scales, q, c, out_0, out_1
                     nc.tensor.transpose(x_banks[k][:, m, u, :], words[:, u : F // 2 : 2], ident[:])
 
         def x_out(k):
-            x_grouped[k] = work.tile([P, 2, P, 4], BF16, name="x_grouped", bufs=3, align_bytes=64)
+            x_grouped[k] = work.tile([P, 2, P, 4], BF16, name="x_grouped", bufs=6, align_bytes=64)
             nc.scalar.copy(out=x_grouped[k][:].bitcast(F32), in_=x_banks[k][:].rearrange("p m u a -> p m a u"))
 
         def quantize_x(k):
@@ -198,7 +214,7 @@ def tile_whole_data_loss_s11_kernel(tc, x, w_words, w_scales, q, c, out_0, out_1
 
         def user_factors(s):
             for eh in range(2):
-                p_banks[s, eh] = bank(eh, [P, HALF])
+                p_banks[s, eh] = bank(4 + eh + (2 if s == 1 else 0), [P, HALF])
                 lhs = x_mx[s // 2]
                 nc.tensor.matmul_mx(
                     out=p_banks[s, eh][:],
@@ -216,12 +232,12 @@ def tile_whole_data_loss_s11_kernel(tc, x, w_words, w_scales, q, c, out_0, out_1
                 in_=src.rearrange("p (b u v r) -> p u b r v", u=2, v=2, r=8),
             )
 
-        def p_out(s):
+        def p_out(s, first=VECTOR_ROUNDS):
             p_sb[s] = work.tile([P, D], F32, name="p_sb", bufs=5)
             p_words[s] = work.tile([P, 2, HALF], BF16, name="p_words", bufs=3)
             for eh in range(2):
                 nc.scalar.copy(out=p_sb[s][:, cols(eh, HALF)], in_=p_banks[s, eh][:])
-            for h in range(VECTOR_ROUNDS, 2):
+            for h in range(first, 2):
                 round_p(s, h, nc.scalar.copy, p_banks[s, h][:])
 
         def round_p_first_half(s):
@@ -229,7 +245,7 @@ def tile_whole_data_loss_s11_kernel(tc, x, w_words, w_scales, q, c, out_0, out_1
                 round_p(s, h, nc.vector.tensor_copy, p_sb[s][:, cols(h, HALF)])
 
         def transpose_p(s):
-            pt_banks[s] = bank(2 + s % 2, [P, 2, 2, P])
+            pt_banks[s] = bank(6 + s % 2, [P, 2, 2, P])
             for h in range(2):
                 words = p_words[s][:, h, :].bitcast(F32)
                 for u in range(2):
@@ -253,7 +269,7 @@ def tile_whole_data_loss_s11_kernel(tc, x, w_words, w_scales, q, c, out_0, out_1
 
         def through_gram(s, pieces):
             for eh in range(2):
-                r_banks[s, eh] = bank(4 + eh, [P, HALF])
+                r_banks[s, eh] = bank(eh + (4 if s >= ALT and s % 2 == 0 else 0), [P, HALF])
             for eh, lo, hi in pieces:
                 for h in range(2):
                     mx_matmul(r_banks[s, eh][:, lo:hi], p_mx[s], cols(h), g_mx[h, eh], slice(lo, hi), start=(h == 0), stop=(h == 1))
@@ -274,7 +290,7 @@ def tile_whole_data_loss_s11_kernel(tc, x, w_words, w_scales, q, c, out_0, out_1
 
         def add_to_loss(src, eh, first, last):
             if first:
-                loss_banks[eh] = bank(6 + eh, [P, 4, P])
+                loss_banks[eh] = bank(2 + eh, [P, 4, P])
             for n in range(4):
                 nc.tensor.matmul(
                     out=loss_banks[eh][:, n, :], lhsT=src[:, cols(n)], rhs=ident[:], is_transpose=True,
@@ -282,72 +298,82 @@ def tile_whole_data_loss_s11_kernel(tc, x, w_words, w_scales, q, c, out_0, out_1
                 )
 
         interleave_q(0, True)
-        nc.vector.tensor_copy(out=c_run[:], in_=c_sb[:].unsqueeze(2).to_broadcast([P, ITEM_PASSES, 8, 4]))
+        nc.scalar.copy(out=c_run[0], in_=c_first[:].unsqueeze(1).to_broadcast([P, 8, 4]))
         interleave_q(0, False)
         for g in range(ITEM_PASSES):
             interleave_q(g + 1, False)
-            quantize_q(g)
-            if g >= 2:
-                quantize_x(2 * g - 4)
-                quantize_x(2 * g - 3)
-            gram_pass(0, 0, g, 0)
-            if g >= 1:
-                x_out(2 * g - 2)
-                x_out(2 * g - 1)
+            weight_q(g)
             if g < 3:
-                transpose_x(2 * g)
-                transpose_x(2 * g + 1)
+                interleave_q(g + 1, True)
+            quantize_q(g)
+            quantize_qc(g)
+            if g == 0:
+                nc.vector.tensor_copy(out=c_rest[:], in_=c_sb[:].unsqueeze(2).to_broadcast([P, ITEM_PASSES - 1, 8, 4]))
+            if g == 3:
+                interleave_q(g + 1, True)
+            gram_pass(0, 0, g, 0)
+            if g >= X_LAG:
+                x_out(2 * (g - X_LAG))
+                x_out(2 * (g - X_LAG) + 1)
+            if g < 2 or g == X_LAG + 1:
+                transpose_x(min(2 * g, 4))
+                transpose_x(min(2 * g, 4) + 1)
+        for k in range(2 * (ITEM_PASSES - X_LAG), 6):
+            x_out(k)
 
-        between = [
-            [lambda: quantize_x(4)],
-            [lambda: quantize_x(5)],
-            [],
-            [lambda: quantize_g(0, 0)],
-        ]
         for g in range(ITEM_PASSES):
-            interleave_q(ITEM_PASSES + g + 1, False)
-            if g < 2:
-                for n in (2 * g, 2 * g + 1):
-                    gram_out(0, 0, n, nc.scalar.copy)
-            quantize_q(ITEM_PASSES + g, between[g])
+            k = ITEM_PASSES + g
+            interleave_q(k + 1, False)
+            interleave_q(k + 1, True)
+            if g == 3:
+                quantize_x(0)
+            quantize_q(k)
             gram_pass(0, 1, g, 4)
-            if g < 2:
-                for earlier in range(g + 1):
-                    gram_pass(1, 0, earlier, 0, (2 * g, 2 * g + 1))
+            if g == G00_AT:
+                for n in range(4):
+                    gram_out(0, 0, n, nc.scalar.copy)
+            if g == W_AT:
+                weight_q(ITEM_PASSES)
+            if g == W_AT + 1:
+                quantize_qc(ITEM_PASSES)
+        if G00_AT == 4:
+            for n in range(4):
+                gram_out(0, 0, n, nc.scalar.copy)
+
+        for n in range(4):
+            gram_out(0, 1, n, nc.scalar.copy)
+        for g in range(ITEM_PASSES):
+            k = ITEM_PASSES + g
+            if g > 0:
+                weight_q(k)
                 if g == 1:
-                    gram_pass(1, 0, 1, 0, (0, 1))
-            else:
-                gram_pass(1, 0, g, 0)
+                    quantize_x(1)
+                else:
+                    quantize_g(0, g - 2)
+                quantize_qc(k)
+            if g >= 1:
+                user_factors(g - 1)
+                p_out(g - 1, FIRST[g - 1])
+            gram_pass(1, 0, g, 0)
 
         engines = (nc.scalar.copy, nc.vector.tensor_copy)
+        for s in range(2):
+            if FIRST[s]:
+                round_p_first_half(s)
         for n in range(4):
-            gram_out(0, 1, n, engines[n % 2])
-        for n in range(4):
-            gram_out(1, 0, n, engines[n % 2])
-        gram_bank(1, 1, 0, 4)
-        user_factors(0)
-        p_out(0)
-        quantize_g(0, 1)
+            gram_out(1, 0, n, engines[G10[n]])
+        if FIRST[2]:
+            round_p_first_half(2)
         quantize_g(1, 0)
-        gram_bank(1, 1, 1, 4)
-        gram_out(1, 1, 0, nc.vector.tensor_copy)
-        round_p_first_half(0)
-        user_factors(1)
-        p_out(1)
-        gram_bank(1, 1, 2, 4)
-        transpose_p(0)
-        gram_out(1, 1, 1, nc.vector.tensor_copy)
-        round_p_first_half(1)
-        user_factors(2)
-        pt_out(0)
-        p_out(2)
-        gram_bank(1, 1, 3, 4)
-        gram_out(1, 1, 2, nc.vector.tensor_copy)
-        quantize_p(0)
-        transpose_p(1)
-        gram_out(1, 1, 3, nc.vector.tensor_copy)
-        round_p_first_half(2)
-        quantize_g(1, 1)
+        for n in range(4):
+            gram_bank(1, 1, n, 0)
+            if n == PT_AT:
+                transpose_p(0)
+                transpose_p(1)
+                pt_out(0)
+                quantize_p(0)
+            gram_out(1, 1, n, engines[G11[n]])
+            quantize_g_bank(1, 1, n)
 
         halves = [(0, 0, HALF), (1, 0, HALF)]
         last = TILES - 1
@@ -363,6 +389,8 @@ def tile_whole_data_loss_s11_kernel(tc, x, w_words, w_scales, q, c, out_0, out_1
                 add_pair(s // 2 - 1, s % 2)
             if s + 1 < TILES:
                 quantize_p(s + 1)
+            if s % 2 == 0 and s // 2 + 2 < TILES // 2:
+                quantize_x(s // 2 + 2)
             through_gram(s, halves)
             if s + 3 < TILES:
                 p_out(s + 3)
@@ -383,7 +411,7 @@ def tile_whole_data_loss_s11_kernel(tc, x, w_words, w_scales, q, c, out_0, out_1
             for s in (last - 1, last):
                 add_to_loss(share[s][:, cols(eh, HALF)], eh, first=False, last=(s == last))
             nc.vector.tensor_reduce(out=sums[:, cols(eh, 4)], in_=loss_banks[eh][:], axis=mybir.AxisListType.X, op=ALU.add)
-        rows = bank(0, [P, P])
+        rows = bank(6, [P, P])
         nc.tensor.transpose(rows[:], sums[:], ident[:])
         loss = keep.tile([32, P], F32, name="loss")
         nc.vector.tensor_scalar(out=loss[:], in0=rows[0:32, :], scalar1=1.0 / M, scalar2=None, op0=ALU.mult)

@@ -15,21 +15,17 @@ FP8X4 = mybir.dt.float8_e4m3fn_x4
 FP4X4 = mybir.dt.float4_e2m1fn_x4
 ALU = mybir.AluOpType
 
-P = 128
+PARTS = 128
 HALF = 512
 ITEM_PASSES = I // 512
-TILES = M // P
-VECTOR_COLUMNS = [384, 64, 0, 192, 256, 256, 256, 256]
-PAIRS = 5
-X_LAG = 1
-PT_AT = 0
-ALT = 10
-FIRST = [0, 0, 0]
-G11 = [1, 1, 1, 1]
-G00_AT = 2
-W_AT = 2
-G10 = [1, 1, 1, 1]
-VECTOR_ROUNDS = 1
+CHUNKS = 2 * ITEM_PASSES
+TILES = M // PARTS
+TILE_PAIRS = TILES // 2
+BLOCKS = HALF // PARTS
+AHEAD = 3
+
+VECTOR_FIRST, VECTOR_EARLY, VECTOR_LATER = 320, 64, 224
+SUMMED_PAIRS = TILE_PAIRS - 1
 
 
 def tile_whole_data_loss_s11_kernel(tc, x, w_words, w_scales, q, c, out_0, out_1):
@@ -43,13 +39,13 @@ def tile_whole_data_loss_s11_kernel(tc, x, w_words, w_scales, q, c, out_0, out_1
         def bank(b, shape):
             return psum.tile(shape, F32, name="bank%d" % b, tag="bank%d" % b)
 
-        def mx_pair(name, width):
-            codes = keep.tile([P, width], U32, name=name + "_codes", align_bytes=64)
-            scales = keep.tile([P, width], U8, name=name + "_scales", align_bytes=64)
+        def mx_operand(name, width):
+            codes = keep.tile([PARTS, width], U32, name=name + "_codes", align_bytes=64)
+            scales = keep.tile([PARTS, width], U8, name=name + "_scales", align_bytes=64)
             return codes, scales
 
-        def quantize(pair, src):
-            nc.vector.quantize_mx(out=pair[0][:].bitcast(FP8X4), scales=pair[1][:], in_=src)
+        def quantize(operand, src):
+            nc.vector.quantize_mx(out=operand[0][:].bitcast(FP8X4), scales=operand[1][:], in_=src)
 
         def mx_matmul(out, lhs, lhs_cols, rhs, rhs_cols, start, stop):
             nc.tensor.matmul_mx(
@@ -62,127 +58,121 @@ def tile_whole_data_loss_s11_kernel(tc, x, w_words, w_scales, q, c, out_0, out_1
                 stop=stop,
             )
 
-        def cols(n, width=P):
+        def cols(n, width=PARTS):
             return slice(n * width, (n + 1) * width)
 
-        c_sb = keep.tile([P, ITEM_PASSES - 1, 4], BF16, name="c_sb")
-        c_view = c.rearrange("(g p j) -> p g j", p=P, j=4)
-        c_first = keep.tile([P, 4], BF16, name="c_first")
+        c_later = keep.tile([PARTS, ITEM_PASSES - 1, 4], BF16, name="c_later")
+        c_view = c.rearrange("(g p j) -> p g j", p=PARTS, j=4)
+        c_first = keep.tile([PARTS, 4], BF16, name="c_first")
         nc.scalar.dma_start(out=c_first[:], in_=c_view[:, 0, :])
 
         q_raw = {}
         x_raw = {}
 
-        def load_q(h, g):
-            q_raw[h, g] = keep.tile([P, 4, HALF], BF16, name="q_raw%d%d" % (h, g))
+        def load_q(k):
+            h, g = divmod(k, ITEM_PASSES)
+            q_raw[k] = keep.tile([PARTS, 4, HALF], BF16, name="q_raw%d" % k)
             rows = q[cols(g, 512), cols(h, HALF)]
-            nc.sync.dma_start(out=q_raw[h, g][:], in_=rows.rearrange("(p j) w -> p j w", j=4))
+            nc.sync.dma_start(out=q_raw[k][:], in_=rows.rearrange("(p j) w -> p j w", j=4))
 
         def load_x(j):
-            x_raw[j] = keep.tile([P, 4, F], BF16, name="x_raw%d" % j)
+            x_raw[j] = keep.tile([PARTS, 4, F], BF16, name="x_raw%d" % j)
             nc.sync.dma_start(out=x_raw[j][:], in_=x[cols(j, 512), :].rearrange("(p m) f -> p m f", m=4))
 
-        ident = keep.tile([P, P], F32, name="ident")
+        ident = keep.tile([PARTS, PARTS], F32, name="ident")
         make_identity(nc, ident[:])
-        w_plane = keep.tile([P, D], U8, name="w_plane", align_bytes=64)
-        nc.gpsimd.memset(w_plane[:].bitcast(I32), 0)
-        sums = keep.tile([P, P], F32, name="sums")
+        w_scale_sb = keep.tile([PARTS, D], U8, name="w_plane", align_bytes=64)
+        nc.gpsimd.memset(w_scale_sb[:].bitcast(I32), 0)
+        sums = keep.tile([PARTS, PARTS], F32, name="sums")
         nc.gpsimd.memset(sums[:], 0.0)
 
-        order = [(0, 0), (0, 1), (0, 2), 0, (0, 3), 1, (1, 0), 2, (1, 1), (1, 2), (1, 3)]
-        for item in order:
-            if isinstance(item, int):
-                load_x(item)
-            else:
-                load_q(*item)
-            if item == (0, 1):
-                nc.sync.dma_start(out=c_sb[:], in_=c_view[:, 1:, :])
-        w_sb = keep.tile([P, 2 * D], U8, name="w_sb", align_bytes=64)
+        for k in range(CHUNKS):
+            load_q(k)
+            if k == 1:
+                nc.sync.dma_start(out=c_later[:], in_=c_view[:, 1:, :])
+            if 1 <= k <= M // 512:
+                load_x(k - 1)
+        w_sb = keep.tile([PARTS, 2 * D], U8, name="w_sb", align_bytes=64)
         nc.sync.dma_start(out=w_sb[:].bitcast(I32), in_=w_words[0].bitcast(I32))
-        for quad in range(4):
+        for n in range(4):
             nc.sync.dma_start(
-                out=w_plane[32 * quad : 32 * quad + 4, :].bitcast(I32),
-                in_=w_scales[0, 4 * quad : 4 * quad + 4, :].bitcast(I32),
+                out=w_scale_sb[32 * n : 32 * n + 4, :].bitcast(I32),
+                in_=w_scales[0, 4 * n : 4 * n + 4, :].bitcast(I32),
             )
 
         q_mx = {}
         qc_mx = {}
         q_grouped = {}
-
         qc_grouped = {}
-        chunks = [(h, g) for h in range(2) for g in range(ITEM_PASSES)]
-        c_rest = keep.tile([P, ITEM_PASSES - 1, 8, 4], BF16, name="c_rest")
-        c_run = [keep.tile([P, 8, 4], BF16, name="c_run")[:]] + [c_rest[:, g, :, :] for g in range(ITEM_PASSES - 1)]
+        c_runs_later = keep.tile([PARTS, ITEM_PASSES - 1, 8, 4], BF16, name="c_runs_later")
+        c_runs_first = keep.tile([PARTS, 8, 4], BF16, name="c_runs_first")
+        c_runs = [c_runs_first[:]] + [c_runs_later[:, g, :, :] for g in range(ITEM_PASSES - 1)]
 
         def interleave_q(k, on_vector):
-            if k >= len(chunks):
-                return
             if k not in q_grouped:
-                q_grouped[k] = work.tile([P, HALF, 4], BF16, name="q_grouped", bufs=5, align_bytes=64)
-            split = VECTOR_COLUMNS[k]
+                q_grouped[k] = work.tile([PARTS, HALF, 4], BF16, name="q_grouped", bufs=5, align_bytes=64)
+            split = VECTOR_FIRST if k == 0 else VECTOR_EARLY if k < 3 else VECTOR_LATER
             lo, hi, copy = (0, split, nc.vector.tensor_copy) if on_vector else (split, HALF, nc.scalar.copy)
-            if hi > lo:
-                copy(
-                    out=q_grouped[k][:, lo:hi, :].rearrange("p (n i) j -> p n j i", i=4),
-                    in_=q_raw[chunks[k]][:, :, lo:hi].rearrange("p j (n i) -> p n j i", i=4),
-                )
+            copy(
+                out=q_grouped[k][:, lo:hi, :].rearrange("p (n i) j -> p n j i", i=4),
+                in_=q_raw[k][:, :, lo:hi].rearrange("p j (n i) -> p n j i", i=4),
+            )
 
         def quantize_q(k):
-            q_mx[chunks[k]] = mx_pair("q%d" % k, HALF)
-            quantize(q_mx[chunks[k]], q_grouped[k][:].rearrange("p w j -> p (w j)"))
+            q_mx[k] = mx_operand("q%d" % k, HALF)
+            quantize(q_mx[k], q_grouped[k][:].rearrange("p w j -> p (w j)"))
 
         def weight_q(k):
-            qc_grouped[k] = work.tile([P, HALF, 4], BF16, name="qc_grouped", align_bytes=64)
-            run = c_run[chunks[k][1]].rearrange("p r j -> p (r j)")
+            qc_grouped[k] = work.tile([PARTS, HALF, 4], BF16, name="qc_grouped", align_bytes=64)
+            run = c_runs[k % ITEM_PASSES].rearrange("p r j -> p (r j)")
             nc.vector.tensor_tensor(
                 out=qc_grouped[k][:].rearrange("p (t b r) j -> p t b (r j)", t=4, r=8),
                 in0=q_grouped[k][:].rearrange("p (b t r) j -> p t b (r j)", t=4, r=8),
-                in1=run.unsqueeze(1).unsqueeze(1).to_broadcast([P, 4, 16, 32]),
+                in1=run.unsqueeze(1).unsqueeze(1).to_broadcast([PARTS, 4, 16, 32]),
                 op=ALU.mult,
             )
 
         def quantize_qc(k):
-            qc_mx[chunks[k]] = mx_pair("qc%d" % k, HALF)
-            quantize(qc_mx[chunks[k]], qc_grouped[k][:].rearrange("p w j -> p (w j)"))
+            qc_mx[k] = mx_operand("qc%d" % k, HALF)
+            quantize(qc_mx[k], qc_grouped[k][:].rearrange("p w j -> p (w j)"))
 
         g_banks = {}
         g_grouped = {}
         g_mx = {}
 
-        def gram_pass(h, eh, g, first_bank, banks=range(4)):
-            for n in banks:
-                if g == 0:
-                    g_banks[h, eh, n] = bank(first_bank + n, [P, 4, P])
-                for t in range(4):
-                    mx_matmul(
-                        g_banks[h, eh, n][:, t, :], qc_mx[h, g], cols(t), q_mx[eh, g], cols(n),
-                        start=(g == 0 and t == 0), stop=(g == ITEM_PASSES - 1 and t == 3),
-                    )
+        def gram_matmul(h, eh, n, t, g, start, stop):
+            lhs, rhs = qc_mx[ITEM_PASSES * h + g], q_mx[ITEM_PASSES * eh + g]
+            mx_matmul(g_banks[h, eh, n][:, t, :], lhs, cols(t), rhs, cols(n), start, stop)
 
-        def gram_bank(h, eh, n, first_bank):
-            g_banks[h, eh, n] = bank(first_bank + n, [P, 4, P])
+        def gram_pass(h, eh, g, first_bank):
+            for n in range(BLOCKS):
+                if g == 0:
+                    g_banks[h, eh, n] = bank(first_bank + n, [PARTS, 4, PARTS])
+                for t in range(4):
+                    gram_matmul(h, eh, n, t, g, start=(g == 0 and t == 0), stop=(g == ITEM_PASSES - 1 and t == 3))
+
+        def gram_bank(h, eh, n):
+            g_banks[h, eh, n] = bank(n, [PARTS, 4, PARTS])
             for t in range(4):
                 for g in range(ITEM_PASSES):
-                    mx_matmul(
-                        g_banks[h, eh, n][:, t, :], qc_mx[h, g], cols(t), q_mx[eh, g], cols(n),
-                        start=(g == 0), stop=(g == ITEM_PASSES - 1),
-                    )
+                    gram_matmul(h, eh, n, t, g, start=(g == 0), stop=(g == ITEM_PASSES - 1))
 
         def gram_out(h, eh, n, copy):
-            if (h, eh) not in g_grouped:
-                g_grouped[h, eh] = work.tile([P, HALF, 4], BF16, name="g_grouped", bufs=3, align_bytes=64)
+            if n == 0:
+                g_grouped[h, eh] = work.tile([PARTS, HALF, 4], BF16, name="g_grouped", bufs=3, align_bytes=64)
             copy(out=g_grouped[h, eh][:, cols(n), :], in_=g_banks[h, eh, n][:].rearrange("p t e -> p e t"))
 
         def quantize_g(h, eh):
-            g_mx[h, eh] = mx_pair("g%d%d" % (h, eh), HALF)
+            g_mx[h, eh] = mx_operand("g%d%d" % (h, eh), HALF)
             quantize(g_mx[h, eh], g_grouped[h, eh][:].rearrange("p e t -> p (e t)"))
 
-        def quantize_g_bank(h, eh, n):
+        def quantize_g_block(h, eh, n):
             if n == 0:
-                g_mx[h, eh] = mx_pair("g%d%d" % (h, eh), HALF)
+                g_mx[h, eh] = mx_operand("g%d%d" % (h, eh), HALF)
             codes, scales = g_mx[h, eh]
             nc.vector.quantize_mx(
-                out=codes[:, cols(n)].bitcast(FP8X4), scales=scales[:, cols(n)],
+                out=codes[:, cols(n)].bitcast(FP8X4),
+                scales=scales[:, cols(n)],
                 in_=g_grouped[h, eh][:, cols(n), :].rearrange("p e t -> p (e t)"),
             )
 
@@ -190,20 +180,20 @@ def tile_whole_data_loss_s11_kernel(tc, x, w_words, w_scales, q, c, out_0, out_1
         x_grouped = {}
         x_mx = {}
 
-        def transpose_x(k):
-            x_banks[k] = bank(4 + k % 4, [P, 2, 2, P])
+        def transpose_x(i):
+            x_banks[i] = bank(4 + i % 4, [PARTS, 2, 2, PARTS])
             for m in range(2):
-                words = x_raw[k // 2][:, 2 * (k % 2) + m, :].bitcast(F32)
+                words = x_raw[i // 2][:, 2 * (i % 2) + m, :].bitcast(F32)
                 for u in range(2):
-                    nc.tensor.transpose(x_banks[k][:, m, u, :], words[:, u : F // 2 : 2], ident[:])
+                    nc.tensor.transpose(x_banks[i][:, m, u, :], words[:, u : F // 2 : 2], ident[:])
 
-        def x_out(k):
-            x_grouped[k] = work.tile([P, 2, P, 4], BF16, name="x_grouped", bufs=6, align_bytes=64)
-            nc.scalar.copy(out=x_grouped[k][:].bitcast(F32), in_=x_banks[k][:].rearrange("p m u a -> p m a u"))
+        def x_out(i):
+            x_grouped[i] = work.tile([PARTS, 2, PARTS, 4], BF16, name="x_grouped", bufs=TILE_PAIRS, align_bytes=64)
+            nc.scalar.copy(out=x_grouped[i][:].bitcast(F32), in_=x_banks[i][:].rearrange("p m u a -> p m a u"))
 
-        def quantize_x(k):
-            x_mx[k] = mx_pair("x%d" % k, 2 * P)
-            quantize(x_mx[k], x_grouped[k][:].rearrange("p m a t -> p (m a t)"))
+        def quantize_x(i):
+            x_mx[i] = mx_operand("x%d" % i, 2 * PARTS)
+            quantize(x_mx[i], x_grouped[i][:].rearrange("p m a t -> p (m a t)"))
 
         p_banks = {}
         p_sb = {}
@@ -212,52 +202,47 @@ def tile_whole_data_loss_s11_kernel(tc, x, w_words, w_scales, q, c, out_0, out_1
         pt_grouped = {}
         p_mx = {}
 
-        def user_factors(s):
+        def user_factors(s, first_bank):
+            codes, scales = x_mx[s // 2]
             for eh in range(2):
-                p_banks[s, eh] = bank(4 + eh + (2 if s == 1 else 0), [P, HALF])
-                lhs = x_mx[s // 2]
+                p_banks[s, eh] = bank(first_bank + eh, [PARTS, HALF])
                 nc.tensor.matmul_mx(
                     out=p_banks[s, eh][:],
-                    lhsT=lhs[0][:, cols(s % 2)].bitcast(FP8X4),
-                    lhsT_scale=lhs[1][:, cols(s % 2)],
+                    lhsT=codes[:, cols(s % 2)].bitcast(FP8X4),
+                    lhsT_scale=scales[:, cols(s % 2)],
                     rhs=w_sb[:, cols(eh, 2 * HALF)].bitcast(FP4X4),
-                    rhs_scale=w_plane[:, cols(eh, HALF)],
+                    rhs_scale=w_scale_sb[:, cols(eh, HALF)],
                     start=True,
                     stop=True,
                 )
 
+        def keep_p(s):
+            p_sb[s] = work.tile([PARTS, D], F32, name="p_sb", bufs=AHEAD + 2)
+            for eh in range(2):
+                nc.scalar.copy(out=p_sb[s][:, cols(eh, HALF)], in_=p_banks[s, eh][:])
+
         def round_p(s, h, copy, src):
+            if s not in p_words:
+                p_words[s] = work.tile([PARTS, 2, HALF], BF16, name="p_words", bufs=AHEAD)
             copy(
                 out=p_words[s][:, h, :].rearrange("p (u b r v) -> p u b r v", u=2, r=8, v=2),
                 in_=src.rearrange("p (b u v r) -> p u b r v", u=2, v=2, r=8),
             )
 
-        def p_out(s, first=VECTOR_ROUNDS):
-            p_sb[s] = work.tile([P, D], F32, name="p_sb", bufs=5)
-            p_words[s] = work.tile([P, 2, HALF], BF16, name="p_words", bufs=3)
-            for eh in range(2):
-                nc.scalar.copy(out=p_sb[s][:, cols(eh, HALF)], in_=p_banks[s, eh][:])
-            for h in range(first, 2):
-                round_p(s, h, nc.scalar.copy, p_banks[s, h][:])
-
-        def round_p_first_half(s):
-            for h in range(VECTOR_ROUNDS):
-                round_p(s, h, nc.vector.tensor_copy, p_sb[s][:, cols(h, HALF)])
-
         def transpose_p(s):
-            pt_banks[s] = bank(6 + s % 2, [P, 2, 2, P])
+            pt_banks[s] = bank(6 + s % 2, [PARTS, 2, 2, PARTS])
             for h in range(2):
                 words = p_words[s][:, h, :].bitcast(F32)
                 for u in range(2):
                     nc.tensor.transpose(pt_banks[s][:, h, u, :], words[:, cols(u)], ident[:])
 
         def pt_out(s):
-            pt_grouped[s] = work.tile([P, 2, P, 4], BF16, name="pt_grouped", align_bytes=64)
+            pt_grouped[s] = work.tile([PARTS, 2, PARTS, 4], BF16, name="pt_grouped", bufs=AHEAD, align_bytes=64)
             nc.scalar.copy(out=pt_grouped[s][:].bitcast(F32), in_=pt_banks[s][:].rearrange("p h u a -> p h a u"))
 
         def quantize_p(s):
-            codes = work.tile([P, 2 * P], U32, name="p_codes", bufs=3, align_bytes=64)
-            scales = work.tile([P, 2 * P], U8, name="p_scales", bufs=3, align_bytes=64)
+            codes = work.tile([PARTS, 2 * PARTS], U32, name="p_codes", bufs=AHEAD, align_bytes=64)
+            scales = work.tile([PARTS, 2 * PARTS], U8, name="p_scales", bufs=AHEAD, align_bytes=64)
             p_mx[s] = (codes, scales)
             quantize(p_mx[s], pt_grouped[s][:].rearrange("p h a t -> p (h a t)"))
 
@@ -265,135 +250,137 @@ def tile_whole_data_loss_s11_kernel(tc, x, w_words, w_scales, q, c, out_0, out_1
         share = {}
         pair_sum = {}
         loss_banks = {}
-        out_tiles = out_0.rearrange("(j p m) e -> j m p e", p=P, m=4)
+        out_tiles = out_0.rearrange("(j p m) e -> j m p e", p=PARTS, m=4)
 
-        def through_gram(s, pieces):
+        def through_gram(s, first_bank):
             for eh in range(2):
-                r_banks[s, eh] = bank(eh + (4 if s >= ALT and s % 2 == 0 else 0), [P, HALF])
-            for eh, lo, hi in pieces:
+                r_banks[s, eh] = bank(first_bank + eh, [PARTS, HALF])
+            for eh in range(2):
                 for h in range(2):
-                    mx_matmul(r_banks[s, eh][:, lo:hi], p_mx[s], cols(h), g_mx[h, eh], slice(lo, hi), start=(h == 0), stop=(h == 1))
+                    mx_matmul(r_banks[s, eh][:], p_mx[s], cols(h), g_mx[h, eh], cols(0, HALF), h == 0, h == 1)
 
         def share_out(s, eh):
             if eh == 0:
-                share[s] = work.tile([P, D], F32, name="share", bufs=5)
+                share[s] = work.tile([PARTS, D], F32, name="share", bufs=5)
             half = cols(eh, HALF)
             nc.vector.tensor_tensor(out=share[s][:, half], in0=r_banks[s, eh][:], in1=p_sb[s][:, half], op=ALU.mult)
 
         def store_share(s, columns):
             nc.sync.dma_start(out=out_tiles[s // 4, s % 4][:, columns], in_=share[s][:, columns])
 
-        def add_pair(k, eh):
+        def add_pair(i, eh):
             half = cols(eh, HALF)
-            pair_sum[k, eh] = work.tile([P, HALF], F32, name="pair_sum")
-            nc.vector.tensor_tensor(out=pair_sum[k, eh][:], in0=share[2 * k][:, half], in1=share[2 * k + 1][:, half], op=ALU.add)
+            pair_sum[i, eh] = work.tile([PARTS, HALF], F32, name="pair_sum")
+            nc.vector.tensor_tensor(
+                out=pair_sum[i, eh][:], in0=share[2 * i][:, half], in1=share[2 * i + 1][:, half], op=ALU.add
+            )
 
-        def add_to_loss(src, eh, first, last):
+        def add_to_loss(src, eh, first=False, final=False):
             if first:
-                loss_banks[eh] = bank(2 + eh, [P, 4, P])
-            for n in range(4):
+                loss_banks[eh] = bank(2 + eh, [PARTS, BLOCKS, PARTS])
+            for n in range(BLOCKS):
                 nc.tensor.matmul(
-                    out=loss_banks[eh][:, n, :], lhsT=src[:, cols(n)], rhs=ident[:], is_transpose=True,
-                    start=(first and n == 0), stop=(last and n == 3),
+                    out=loss_banks[eh][:, n, :],
+                    lhsT=src[:, cols(n)],
+                    rhs=ident[:],
+                    is_transpose=True,
+                    start=(first and n == 0),
+                    stop=(final and n == BLOCKS - 1),
                 )
 
+        on_scalar, on_vector = nc.scalar.copy, nc.vector.tensor_copy
+
         interleave_q(0, True)
-        nc.scalar.copy(out=c_run[0], in_=c_first[:].unsqueeze(1).to_broadcast([P, 8, 4]))
+        nc.scalar.copy(out=c_runs_first[:], in_=c_first[:].unsqueeze(1).to_broadcast([PARTS, 8, 4]))
         interleave_q(0, False)
         for g in range(ITEM_PASSES):
+            final_pass = g == ITEM_PASSES - 1
             interleave_q(g + 1, False)
             weight_q(g)
-            if g < 3:
+            if not final_pass:
                 interleave_q(g + 1, True)
             quantize_q(g)
             quantize_qc(g)
             if g == 0:
-                nc.vector.tensor_copy(out=c_rest[:], in_=c_sb[:].unsqueeze(2).to_broadcast([P, ITEM_PASSES - 1, 8, 4]))
-            if g == 3:
+                spread = c_later[:].unsqueeze(2).to_broadcast([PARTS, ITEM_PASSES - 1, 8, 4])
+                nc.vector.tensor_copy(out=c_runs_later[:], in_=spread)
+            if final_pass:
                 interleave_q(g + 1, True)
+            if not final_pass:
+                transpose_x(2 * g)
+                transpose_x(2 * g + 1)
             gram_pass(0, 0, g, 0)
-            if g >= X_LAG:
-                x_out(2 * (g - X_LAG))
-                x_out(2 * (g - X_LAG) + 1)
-            if g < 2 or g == X_LAG + 1:
-                transpose_x(min(2 * g, 4))
-                transpose_x(min(2 * g, 4) + 1)
-        for k in range(2 * (ITEM_PASSES - X_LAG), 6):
-            x_out(k)
-
-        for g in range(ITEM_PASSES):
-            k = ITEM_PASSES + g
-            interleave_q(k + 1, False)
-            interleave_q(k + 1, True)
-            if g == 3:
-                quantize_x(0)
-            quantize_q(k)
-            gram_pass(0, 1, g, 4)
-            if g == G00_AT:
-                for n in range(4):
-                    gram_out(0, 0, n, nc.scalar.copy)
-            if g == W_AT:
-                weight_q(ITEM_PASSES)
-            if g == W_AT + 1:
-                quantize_qc(ITEM_PASSES)
-        if G00_AT == 4:
-            for n in range(4):
-                gram_out(0, 0, n, nc.scalar.copy)
-
-        for n in range(4):
-            gram_out(0, 1, n, nc.scalar.copy)
-        for g in range(ITEM_PASSES):
-            k = ITEM_PASSES + g
             if g > 0:
-                weight_q(k)
-                if g == 1:
-                    quantize_x(1)
-                else:
-                    quantize_g(0, g - 2)
-                quantize_qc(k)
-            if g >= 1:
-                user_factors(g - 1)
-                p_out(g - 1, FIRST[g - 1])
-            gram_pass(1, 0, g, 0)
+                x_out(2 * g - 2)
+                x_out(2 * g - 1)
 
-        engines = (nc.scalar.copy, nc.vector.tensor_copy)
-        for s in range(2):
-            if FIRST[s]:
-                round_p_first_half(s)
-        for n in range(4):
-            gram_out(1, 0, n, engines[G10[n]])
-        if FIRST[2]:
-            round_p_first_half(2)
+        for k in range(ITEM_PASSES, CHUNKS):
+            if k + 1 < CHUNKS:
+                interleave_q(k + 1, False)
+                interleave_q(k + 1, True)
+            else:
+                weight_q(ITEM_PASSES)
+            quantize_q(k)
+            gram_pass(0, 1, k - ITEM_PASSES, 4)
+            if k + 2 == CHUNKS:
+                for n in range(BLOCKS):
+                    gram_out(0, 0, n, on_scalar)
+
+        quantize_x(0)
+        quantize_qc(ITEM_PASSES)
+        for n in range(BLOCKS):
+            gram_out(0, 1, n, on_scalar)
+        gram_pass(1, 0, 0, 0)
+        for s in range(AHEAD):
+            k = ITEM_PASSES + 1 + s
+            weight_q(k)
+            if s == 1:
+                quantize_x(1)
+            quantize_qc(k)
+            user_factors(s, 4 + 2 * (s % 2))
+            keep_p(s)
+            for h in range(2):
+                round_p(s, h, on_scalar, p_banks[s, h][:])
+            gram_pass(1, 0, s + 1, 0)
+
+        quantize_g(0, 0)
+        transpose_p(0)
+        transpose_p(1)
+        for n in range(BLOCKS):
+            gram_out(1, 0, n, on_vector)
+        pt_out(0)
+        quantize_g(0, 1)
+        for i in range(2, TILE_PAIRS):
+            quantize_x(i)
+        quantize_p(0)
         quantize_g(1, 0)
-        for n in range(4):
-            gram_bank(1, 1, n, 0)
-            if n == PT_AT:
-                transpose_p(0)
-                transpose_p(1)
-                pt_out(0)
-                quantize_p(0)
-            gram_out(1, 1, n, engines[G11[n]])
-            quantize_g_bank(1, 1, n)
+        pt_out(1)
+        for n in range(BLOCKS):
+            gram_bank(1, 1, n)
+            if n == 2:
+                quantize_p(1)
+            gram_out(1, 1, n, on_scalar if n < 2 else on_vector)
+            if n > 0:
+                quantize_g_block(1, 1, n - 1)
+        quantize_g_block(1, 1, BLOCKS - 1)
 
-        halves = [(0, 0, HALF), (1, 0, HALF)]
         last = TILES - 1
         for s in range(TILES):
-            paired = 2 <= s < 2 * PAIRS + 2
-            if s + 3 < TILES:
-                user_factors(s + 3)
-            if s + 1 < TILES:
+            pair, pair_half = divmod(s - 2, 2)
+            if s + AHEAD < TILES:
+                user_factors(s + AHEAD, 4)
+            if 0 < s < last:
                 pt_out(s + 1)
-            if 0 < s and s + 2 < TILES:
-                round_p_first_half(s + 2)
-            if paired:
-                add_pair(s // 2 - 1, s % 2)
-            if s + 1 < TILES:
+            if AHEAD <= s + 2 < TILES:
+                round_p(s + 2, 0, on_vector, p_sb[s + 2][:, cols(0, HALF)])
+            if pair >= 0:
+                add_pair(pair, pair_half)
+            if 0 < s < last:
                 quantize_p(s + 1)
-            if s % 2 == 0 and s // 2 + 2 < TILES // 2:
-                quantize_x(s // 2 + 2)
-            through_gram(s, halves)
-            if s + 3 < TILES:
-                p_out(s + 3)
+            through_gram(s, 4 if s == last - 1 else 0)
+            if s + AHEAD < TILES:
+                keep_p(s + AHEAD)
+                round_p(s + AHEAD, 1, on_scalar, p_banks[s + AHEAD, 1][:])
             share_out(s, 0)
             if s == last:
                 store_share(s, cols(0, HALF))
@@ -401,18 +388,19 @@ def tile_whole_data_loss_s11_kernel(tc, x, w_words, w_scales, q, c, out_0, out_1
             store_share(s, cols(1, HALF) if s == last else cols(0, D))
             if s + 2 < TILES:
                 transpose_p(s + 2)
-            if paired:
-                add_to_loss(pair_sum[s // 2 - 1, s % 2], s % 2, first=(s < 4), last=False)
-            if s - 1 >= 2 * PAIRS and s < last:
-                for eh in range(2):
-                    add_to_loss(share[s - 1][:, cols(eh, HALF)], eh, first=False, last=False)
+            if pair >= 0 and s < last:
+                add_to_loss(pair_sum[pair, pair_half], pair_half, first=(pair == 0))
 
         for eh in range(2):
-            for s in (last - 1, last):
-                add_to_loss(share[s][:, cols(eh, HALF)], eh, first=False, last=(s == last))
-            nc.vector.tensor_reduce(out=sums[:, cols(eh, 4)], in_=loss_banks[eh][:], axis=mybir.AxisListType.X, op=ALU.add)
-        rows = bank(6, [P, P])
+            add_to_loss(share[last - 1][:, cols(eh, HALF)], eh)
+            if eh == 0:
+                add_to_loss(pair_sum[SUMMED_PAIRS - 1, 1], 1)
+            add_to_loss(share[last][:, cols(eh, HALF)], eh, final=True)
+            nc.vector.tensor_reduce(
+                out=sums[:, cols(eh, BLOCKS)], in_=loss_banks[eh][:], axis=mybir.AxisListType.X, op=ALU.add
+            )
+        rows = bank(6, [PARTS, PARTS])
         nc.tensor.transpose(rows[:], sums[:], ident[:])
-        loss = keep.tile([32, P], F32, name="loss")
+        loss = keep.tile([32, PARTS], F32, name="loss")
         nc.vector.tensor_scalar(out=loss[:], in0=rows[0:32, :], scalar1=1.0 / M, scalar2=None, op0=ALU.mult)
-        nc.sync.dma_start(out=out_1.rearrange("(n p) -> n p", p=P), in_=loss[0:8, :])
+        nc.sync.dma_start(out=out_1.rearrange("(n p) -> n p", p=PARTS), in_=loss[0 : D // PARTS, :])

from contextlib import ExitStack

import concourse.mybir as mybir
from concourse.masks import make_identity

M, F, D, I = 1536, 512, 1024, 2048
FLOPS = 2 * M * F * D + 2 * I * D * D + 2 * M * D * D

F32 = mybir.dt.float32
BF16 = mybir.dt.bfloat16
I32 = mybir.dt.int32
U32 = mybir.dt.uint32
U8 = mybir.dt.uint8
FP8X4 = mybir.dt.float8_e4m3fn_x4
FP4X4 = mybir.dt.float4_e2m1fn_x4
ALU = mybir.AluOpType

PARTS = 128
HALF = 512
ITEM_PASSES = I // 512
CHUNKS = 2 * ITEM_PASSES
TILES = M // PARTS
TILE_PAIRS = TILES // 2
BLOCKS = HALF // PARTS
AHEAD = 3

VECTOR_FIRST, VECTOR_EARLY, VECTOR_LATER = 320, 64, 224
SUMMED_PAIRS = TILE_PAIRS - 1


def tile_whole_data_loss_s11_kernel(tc, x, w_words, w_scales, q, c, out_0, out_1):
    nc = tc.nc
    with ExitStack() as ctx:
        keep = ctx.enter_context(tc.tile_pool(name="keep", bufs=1))
        work = ctx.enter_context(tc.tile_pool(name="work", bufs=2))
        psum = ctx.enter_context(tc.psum_pool(name="psum", bufs=1))
        ctx.enter_context(tc.manual_schedule())

        def bank(b, shape):
            return psum.tile(shape, F32, name="bank%d" % b, tag="bank%d" % b)

        def mx_operand(name, width):
            codes = keep.tile([PARTS, width], U32, name=name + "_codes", align_bytes=64)
            scales = keep.tile([PARTS, width], U8, name=name + "_scales", align_bytes=64)
            return codes, scales

        def quantize(operand, src):
            nc.vector.quantize_mx(out=operand[0][:].bitcast(FP8X4), scales=operand[1][:], in_=src)

        def mx_matmul(out, lhs, lhs_cols, rhs, rhs_cols, start, stop):
            nc.tensor.matmul_mx(
                out=out,
                lhsT=lhs[0][:, lhs_cols].bitcast(FP8X4),
                lhsT_scale=lhs[1][:, lhs_cols],
                rhs=rhs[0][:, rhs_cols].bitcast(FP8X4),
                rhs_scale=rhs[1][:, rhs_cols],
                start=start,
                stop=stop,
            )

        def cols(n, width=PARTS):
            return slice(n * width, (n + 1) * width)

        c_later = keep.tile([PARTS, ITEM_PASSES - 1, 4], BF16, name="c_later")
        c_view = c.rearrange("(g p j) -> p g j", p=PARTS, j=4)
        c_first = keep.tile([PARTS, 4], BF16, name="c_first")
        nc.scalar.dma_start(out=c_first[:], in_=c_view[:, 0, :])

        q_raw = {}
        x_raw = {}

        def load_q(k):
            h, g = divmod(k, ITEM_PASSES)
            q_raw[k] = keep.tile([PARTS, 4, HALF], BF16, name="q_raw%d" % k)
            rows = q[cols(g, 512), cols(h, HALF)]
            nc.sync.dma_start(out=q_raw[k][:], in_=rows.rearrange("(p j) w -> p j w", j=4))

        def load_x(j):
            x_raw[j] = keep.tile([PARTS, 4, F], BF16, name="x_raw%d" % j)
            nc.sync.dma_start(out=x_raw[j][:], in_=x[cols(j, 512), :].rearrange("(p m) f -> p m f", m=4))

        ident = keep.tile([PARTS, PARTS], F32, name="ident")
        make_identity(nc, ident[:])
        w_scale_sb = keep.tile([PARTS, D], U8, name="w_plane", align_bytes=64)
        nc.gpsimd.memset(w_scale_sb[:].bitcast(I32), 0)
        sums = keep.tile([PARTS, PARTS], F32, name="sums")
        nc.gpsimd.memset(sums[:], 0.0)

        for k in range(CHUNKS):
            load_q(k)
            if k == 1:
                nc.sync.dma_start(out=c_later[:], in_=c_view[:, 1:, :])
            if 1 <= k <= M // 512:
                load_x(k - 1)
        w_sb = keep.tile([PARTS, 2 * D], U8, name="w_sb", align_bytes=64)
        nc.sync.dma_start(out=w_sb[:].bitcast(I32), in_=w_words[0].bitcast(I32))
        for n in range(4):
            nc.sync.dma_start(
                out=w_scale_sb[32 * n : 32 * n + 4, :].bitcast(I32),
                in_=w_scales[0, 4 * n : 4 * n + 4, :].bitcast(I32),
            )

        q_mx = {}
        qc_mx = {}
        q_grouped = {}
        qc_grouped = {}
        c_runs_later = keep.tile([PARTS, ITEM_PASSES - 1, 8, 4], BF16, name="c_runs_later")
        c_runs_first = keep.tile([PARTS, 8, 4], BF16, name="c_runs_first")
        c_runs = [c_runs_first[:]] + [c_runs_later[:, g, :, :] for g in range(ITEM_PASSES - 1)]

        def interleave_q(k, on_vector):
            if k not in q_grouped:
                q_grouped[k] = work.tile([PARTS, HALF, 4], BF16, name="q_grouped", bufs=5, align_bytes=64)
            split = VECTOR_FIRST if k == 0 else VECTOR_EARLY if k < 3 else VECTOR_LATER
            lo, hi, copy = (0, split, nc.vector.tensor_copy) if on_vector else (split, HALF, nc.scalar.copy)
            copy(
                out=q_grouped[k][:, lo:hi, :].rearrange("p (n i) j -> p n j i", i=4),
                in_=q_raw[k][:, :, lo:hi].rearrange("p j (n i) -> p n j i", i=4),
            )

        def quantize_q(k):
            q_mx[k] = mx_operand("q%d" % k, HALF)
            quantize(q_mx[k], q_grouped[k][:].rearrange("p w j -> p (w j)"))

        def weight_q(k):
            qc_grouped[k] = work.tile([PARTS, HALF, 4], BF16, name="qc_grouped", align_bytes=64)
            run = c_runs[k % ITEM_PASSES].rearrange("p r j -> p (r j)")
            nc.vector.tensor_tensor(
                out=qc_grouped[k][:].rearrange("p (t b r) j -> p t b (r j)", t=4, r=8),
                in0=q_grouped[k][:].rearrange("p (b t r) j -> p t b (r j)", t=4, r=8),
                in1=run.unsqueeze(1).unsqueeze(1).to_broadcast([PARTS, 4, 16, 32]),
                op=ALU.mult,
            )

        def quantize_qc(k):
            qc_mx[k] = mx_operand("qc%d" % k, HALF)
            quantize(qc_mx[k], qc_grouped[k][:].rearrange("p w j -> p (w j)"))

        g_banks = {}
        g_grouped = {}
        g_mx = {}

        def gram_matmul(h, eh, n, t, g, start, stop):
            lhs, rhs = qc_mx[ITEM_PASSES * h + g], q_mx[ITEM_PASSES * eh + g]
            mx_matmul(g_banks[h, eh, n][:, t, :], lhs, cols(t), rhs, cols(n), start, stop)

        def gram_pass(h, eh, g, first_bank):
            for n in range(BLOCKS):
                if g == 0:
                    g_banks[h, eh, n] = bank(first_bank + n, [PARTS, 4, PARTS])
                for t in range(4):
                    gram_matmul(h, eh, n, t, g, start=(g == 0 and t == 0), stop=(g == ITEM_PASSES - 1 and t == 3))

        def gram_bank(h, eh, n):
            g_banks[h, eh, n] = bank(n, [PARTS, 4, PARTS])
            for t in range(4):
                for g in range(ITEM_PASSES):
                    gram_matmul(h, eh, n, t, g, start=(g == 0), stop=(g == ITEM_PASSES - 1))

        def gram_out(h, eh, n, copy):
            if n == 0:
                g_grouped[h, eh] = work.tile([PARTS, HALF, 4], BF16, name="g_grouped", bufs=3, align_bytes=64)
            copy(out=g_grouped[h, eh][:, cols(n), :], in_=g_banks[h, eh, n][:].rearrange("p t e -> p e t"))

        def quantize_g(h, eh):
            g_mx[h, eh] = mx_operand("g%d%d" % (h, eh), HALF)
            quantize(g_mx[h, eh], g_grouped[h, eh][:].rearrange("p e t -> p (e t)"))

        def quantize_g_block(h, eh, n):
            if n == 0:
                g_mx[h, eh] = mx_operand("g%d%d" % (h, eh), HALF)
            codes, scales = g_mx[h, eh]
            nc.vector.quantize_mx(
                out=codes[:, cols(n)].bitcast(FP8X4),
                scales=scales[:, cols(n)],
                in_=g_grouped[h, eh][:, cols(n), :].rearrange("p e t -> p (e t)"),
            )

        x_banks = {}
        x_grouped = {}
        x_mx = {}

        def transpose_x(i):
            x_banks[i] = bank(4 + i % 4, [PARTS, 2, 2, PARTS])
            for m in range(2):
                words = x_raw[i // 2][:, 2 * (i % 2) + m, :].bitcast(F32)
                for u in range(2):
                    nc.tensor.transpose(x_banks[i][:, m, u, :], words[:, u : F // 2 : 2], ident[:])

        def x_out(i):
            x_grouped[i] = work.tile([PARTS, 2, PARTS, 4], BF16, name="x_grouped", bufs=TILE_PAIRS, align_bytes=64)
            nc.scalar.copy(out=x_grouped[i][:].bitcast(F32), in_=x_banks[i][:].rearrange("p m u a -> p m a u"))

        def quantize_x(i):
            x_mx[i] = mx_operand("x%d" % i, 2 * PARTS)
            quantize(x_mx[i], x_grouped[i][:].rearrange("p m a t -> p (m a t)"))

        p_banks = {}
        p_sb = {}
        p_words = {}
        pt_banks = {}
        pt_grouped = {}
        p_mx = {}

        def user_factors(s, first_bank):
            codes, scales = x_mx[s // 2]
            for eh in range(2):
                p_banks[s, eh] = bank(first_bank + eh, [PARTS, HALF])
                nc.tensor.matmul_mx(
                    out=p_banks[s, eh][:],
                    lhsT=codes[:, cols(s % 2)].bitcast(FP8X4),
                    lhsT_scale=scales[:, cols(s % 2)],
                    rhs=w_sb[:, cols(eh, 2 * HALF)].bitcast(FP4X4),
                    rhs_scale=w_scale_sb[:, cols(eh, HALF)],
                    start=True,
                    stop=True,
                )

        def keep_p(s):
            p_sb[s] = work.tile([PARTS, D], F32, name="p_sb", bufs=AHEAD + 2)
            for eh in range(2):
                nc.scalar.copy(out=p_sb[s][:, cols(eh, HALF)], in_=p_banks[s, eh][:])

        def round_p(s, h, copy, src):
            if s not in p_words:
                p_words[s] = work.tile([PARTS, 2, HALF], BF16, name="p_words", bufs=AHEAD)
            copy(
                out=p_words[s][:, h, :].rearrange("p (u b r v) -> p u b r v", u=2, r=8, v=2),
                in_=src.rearrange("p (b u v r) -> p u b r v", u=2, v=2, r=8),
            )

        def transpose_p(s):
            pt_banks[s] = bank(6 + s % 2, [PARTS, 2, 2, PARTS])
            for h in range(2):
                words = p_words[s][:, h, :].bitcast(F32)
                for u in range(2):
                    nc.tensor.transpose(pt_banks[s][:, h, u, :], words[:, cols(u)], ident[:])

        def pt_out(s):
            pt_grouped[s] = work.tile([PARTS, 2, PARTS, 4], BF16, name="pt_grouped", bufs=AHEAD, align_bytes=64)
            nc.scalar.copy(out=pt_grouped[s][:].bitcast(F32), in_=pt_banks[s][:].rearrange("p h u a -> p h a u"))

        def quantize_p(s):
            codes = work.tile([PARTS, 2 * PARTS], U32, name="p_codes", bufs=AHEAD, align_bytes=64)
            scales = work.tile([PARTS, 2 * PARTS], U8, name="p_scales", bufs=AHEAD, align_bytes=64)
            p_mx[s] = (codes, scales)
            quantize(p_mx[s], pt_grouped[s][:].rearrange("p h a t -> p (h a t)"))

        r_banks = {}
        share = {}
        pair_sum = {}
        loss_banks = {}
        out_tiles = out_0.rearrange("(j p m) e -> j m p e", p=PARTS, m=4)

        def through_gram(s, first_bank):
            for eh in range(2):
                r_banks[s, eh] = bank(first_bank + eh, [PARTS, HALF])
            for eh in range(2):
                for h in range(2):
                    mx_matmul(r_banks[s, eh][:], p_mx[s], cols(h), g_mx[h, eh], cols(0, HALF), h == 0, h == 1)

        def share_out(s, eh):
            if eh == 0:
                share[s] = work.tile([PARTS, D], F32, name="share", bufs=5)
            half = cols(eh, HALF)
            nc.vector.tensor_tensor(out=share[s][:, half], in0=r_banks[s, eh][:], in1=p_sb[s][:, half], op=ALU.mult)

        def store_share(s, columns):
            nc.sync.dma_start(out=out_tiles[s // 4, s % 4][:, columns], in_=share[s][:, columns])

        def add_pair(i, eh):
            half = cols(eh, HALF)
            pair_sum[i, eh] = work.tile([PARTS, HALF], F32, name="pair_sum")
            nc.vector.tensor_tensor(
                out=pair_sum[i, eh][:], in0=share[2 * i][:, half], in1=share[2 * i + 1][:, half], op=ALU.add
            )

        def add_to_loss(src, eh, first=False, final=False):
            if first:
                loss_banks[eh] = bank(2 + eh, [PARTS, BLOCKS, PARTS])
            for n in range(BLOCKS):
                nc.tensor.matmul(
                    out=loss_banks[eh][:, n, :],
                    lhsT=src[:, cols(n)],
                    rhs=ident[:],
                    is_transpose=True,
                    start=(first and n == 0),
                    stop=(final and n == BLOCKS - 1),
                )

        on_scalar, on_vector = nc.scalar.copy, nc.vector.tensor_copy

        interleave_q(0, True)
        nc.scalar.copy(out=c_runs_first[:], in_=c_first[:].unsqueeze(1).to_broadcast([PARTS, 8, 4]))
        interleave_q(0, False)
        for g in range(ITEM_PASSES):
            final_pass = g == ITEM_PASSES - 1
            interleave_q(g + 1, False)
            weight_q(g)
            if not final_pass:
                interleave_q(g + 1, True)
            quantize_q(g)
            quantize_qc(g)
            if g == 0:
                spread = c_later[:].unsqueeze(2).to_broadcast([PARTS, ITEM_PASSES - 1, 8, 4])
                nc.vector.tensor_copy(out=c_runs_later[:], in_=spread)
            if final_pass:
                interleave_q(g + 1, True)
            if not final_pass:
                transpose_x(2 * g)
                transpose_x(2 * g + 1)
            gram_pass(0, 0, g, 0)
            if g > 0:
                x_out(2 * g - 2)
                x_out(2 * g - 1)

        for k in range(ITEM_PASSES, CHUNKS):
            if k + 1 < CHUNKS:
                interleave_q(k + 1, False)
                interleave_q(k + 1, True)
            else:
                weight_q(ITEM_PASSES)
            quantize_q(k)
            gram_pass(0, 1, k - ITEM_PASSES, 4)
            if k + 2 == CHUNKS:
                for n in range(BLOCKS):
                    gram_out(0, 0, n, on_scalar)

        quantize_x(0)
        quantize_qc(ITEM_PASSES)
        for n in range(BLOCKS):
            gram_out(0, 1, n, on_scalar)
        gram_pass(1, 0, 0, 0)
        for s in range(AHEAD):
            k = ITEM_PASSES + 1 + s
            weight_q(k)
            if s == 1:
                quantize_x(1)
            quantize_qc(k)
            user_factors(s, 4 + 2 * (s % 2))
            keep_p(s)
            for h in range(2):
                round_p(s, h, on_scalar, p_banks[s, h][:])
            gram_pass(1, 0, s + 1, 0)

        quantize_g(0, 0)
        transpose_p(0)
        transpose_p(1)
        for n in range(BLOCKS):
            gram_out(1, 0, n, on_vector)
        pt_out(0)
        quantize_g(0, 1)
        for i in range(2, TILE_PAIRS):
            quantize_x(i)
        quantize_p(0)
        quantize_g(1, 0)
        pt_out(1)
        for n in range(BLOCKS):
            gram_bank(1, 1, n)
            if n == 2:
                quantize_p(1)
            gram_out(1, 1, n, on_scalar if n < 2 else on_vector)
            if n > 0:
                quantize_g_block(1, 1, n - 1)
        quantize_g_block(1, 1, BLOCKS - 1)

        last = TILES - 1
        for s in range(TILES):
            pair, pair_half = divmod(s - 2, 2)
            if s + AHEAD < TILES:
                user_factors(s + AHEAD, 4)
            if 0 < s < last:
                pt_out(s + 1)
            if AHEAD <= s + 2 < TILES:
                round_p(s + 2, 0, on_vector, p_sb[s + 2][:, cols(0, HALF)])
            if pair >= 0:
                add_pair(pair, pair_half)
            if 0 < s < last:
                quantize_p(s + 1)
            through_gram(s, 4 if s == last - 1 else 0)
            if s + AHEAD < TILES:
                keep_p(s + AHEAD)
                round_p(s + AHEAD, 1, on_scalar, p_banks[s + AHEAD, 1][:])
            share_out(s, 0)
            if s == last:
                store_share(s, cols(0, HALF))
            share_out(s, 1)
            store_share(s, cols(1, HALF) if s == last else cols(0, D))
            if s + 2 < TILES:
                transpose_p(s + 2)
            if pair >= 0 and s < last:
                add_to_loss(pair_sum[pair, pair_half], pair_half, first=(pair == 0))

        for eh in range(2):
            add_to_loss(share[last - 1][:, cols(eh, HALF)], eh)
            if eh == 0:
                add_to_loss(pair_sum[SUMMED_PAIRS - 1, 1], 1)
            add_to_loss(share[last][:, cols(eh, HALF)], eh, final=True)
            nc.vector.tensor_reduce(
                out=sums[:, cols(eh, BLOCKS)], in_=loss_banks[eh][:], axis=mybir.AxisListType.X, op=ALU.add
            )
        rows = bank(6, [PARTS, PARTS])
        nc.tensor.transpose(rows[:], sums[:], ident[:])
        loss = keep.tile([32, PARTS], F32, name="loss")
        nc.vector.tensor_scalar(out=loss[:], in0=rows[0:32, :], scalar1=1.0 / M, scalar2=None, op0=ALU.mult)
        nc.sync.dma_start(out=out_1.rearrange("(n p) -> n p", p=PARTS), in_=loss[0 : D // PARTS, :])
